import numpy as np
import ml_dtypes


def mxq(x, axis, fmt="e4m3"):
    dtype, down = {"e4m3": (ml_dtypes.float8_e4m3fn, 7), "e5m2": (ml_dtypes.float8_e5m2, 14)}[fmt]
    v = np.moveaxis(np.asarray(x, np.float32).astype(ml_dtypes.bfloat16).astype(np.float64), axis, -1)
    blocks = v.reshape(v.shape[:-1] + (-1, 32))
    amax = np.abs(blocks).max(-1, keepdims=True)
    byte = np.maximum(np.where(amax > 0, np.frexp(amax)[1] - 1 + 127, 0) - down, 1)
    scale = np.exp2(byte - 127.0)
    codes = (blocks / scale).astype(np.float32).astype(dtype).astype(np.float64)
    return np.moveaxis((codes * scale).reshape(v.shape), -1, axis)


WIDE = False


def mx_kscale(k):
    if not WIDE:
        return np.ones(k)
    levels = np.array([10, -10, 5, -5, 0])
    if k % 512:
        return np.exp2(np.random.permutation(np.resize(levels, k // 32))).repeat(32)
    a = np.empty((k // 512, 16))
    for p in range(k // 512):
        a[p, :8] = np.random.permutation(np.resize(levels, 8))
        for g in range(8):
            far = levels[np.abs(levels - a[p, g]) >= 10]
            a[p, g + 8] = far[np.random.randint(len(far))]
    return np.exp2(a.ravel()).repeat(32)


def f64(x):
    return np.asarray(x).astype(np.float64)


def striped(idx):
    return np.tile(idx.reshape(-1, 16).T, (8, 1)).astype(np.uint16)


def unstriped(offs):
    return offs[:16].T.reshape(-1).astype(np.int64)


def striped8(idx):
    return np.concatenate([x.reshape(-1, 16).T for x in idx]).astype(np.uint16)


def runs(offs, k):
    lists = np.stack([offs[16 * r : 16 * r + 16].T.reshape(-1) for r in range(8)]).astype(np.int64)
    return lists[np.arange(k) % 512 // 64]


def pack_weight(w):
    k, n = w.shape
    w = f64(np.asarray(w, np.float32).astype(ml_dtypes.bfloat16)).reshape(k // 32, 32, n)
    amax = np.abs(w).max(1)
    byte = np.clip(np.where(amax > 0, np.frexp(amax)[1] - 1 + 127 - 7, 1), 1, 254)
    scaled = (w * np.exp2(127.0 - byte)[:, None, :]).reshape(k, n).astype(np.float32)
    words = np.ascontiguousarray(scaled.reshape(k // 512, 128, 4, n).transpose(0, 1, 3, 2)).astype(ml_dtypes.float8_e4m3fn).view(np.uint8)
    return words, np.ascontiguousarray(byte.astype(np.uint8).reshape(k // 512, 16, n))


def unpack_weight(words, scales):
    g, p, n, _ = words.shape
    vals = np.ascontiguousarray(words).view(ml_dtypes.float8_e4m3fn).astype(np.float64) * np.repeat(np.exp2(scales.astype(np.float64) - 127.0), 8, axis=1)[..., None]
    return vals.transpose(0, 1, 3, 2).reshape(g * 512, n)


K, T, S, G, H, U = 512, 1024, 256, 2048, 512, 1024


def setup_inputs():
    n = np.random.standard_normal
    s = mx_kscale(K)[:, None]
    packed_xT = pack_weight(n((K, T)) * s)
    packed_dT = pack_weight(n((K, G)) / s)
    return {
        "x_words": packed_xT[0],
        "x_scales": packed_xT[1],
        "d_words": packed_dT[0],
        "d_scales": packed_dT[1],
        "gs": (np.random.uniform(0.5, 1.5, (K, 1)) * s).astype(np.float32),
        "offs": striped8(np.random.randint(0, T, (8, S))),
        "k1": striped8(np.random.randint(0, G, (8, H))),
        "hz": striped8(np.random.randint(0, T, (8, S))),
        "k2": striped8(np.random.randint(0, G, (8, H))),
        "n1": striped(np.random.permutation(S)),
        "n2": striped(np.random.permutation(S)),
        "n3": striped(np.random.permutation(S)),
        "k3": striped8(np.random.randint(0, G, (8, H))),
        "n4": striped(np.random.permutation(U)[:S]),
        "n5": striped(np.random.permutation(S)),
    }


def reference(x_words, x_scales, d_words, d_scales, gs, offs, k1, hz, k2, n1, n2, n3, k3, n4, n5):
    d_k3 = unpack_weight(d_words, d_scales)[np.arange(K)[:, None], runs(k3, K)]
    d_k1 = unpack_weight(d_words, d_scales)[np.arange(K)[:, None], runs(k1, K)]
    xq = unpack_weight(x_words, x_scales)[np.arange(K)[:, None], runs(offs, K)]
    d_k2 = unpack_weight(d_words, d_scales)[np.arange(K)[:, None], runs(k2, K)]
    x_hz = unpack_weight(x_words, x_scales)[np.arange(K)[:, None], runs(hz, K)]
    h = 0.0625 * (d_k1.T @ xq + d_k2.T @ x_hz)
    ds = np.zeros((H, S))
    ds[:, unstriped(n1)] = h
    st = np.minimum(ds, h[:, unstriped(n2)])
    z = f64(gs) * (st - st[:, unstriped(n3)])
    h2 = 0.0625 * ((d_k3.T @ mxq(z, 0, "e4m3")))
    nw = np.maximum(h2, h2[:, unstriped(n5)])
    out = np.zeros((H, U))
    out[:, unstriped(n4)] = nw
    return out

@@ -1,0 +1,189 @@
+from contextlib import ExitStack
+
+import concourse.mybir as mybir
+
+K, T, S, G, H, U = 512, 1024, 256, 2048, 512, 1024
+FLOPS = 3 * 2 * K * H * S
+
+F32 = mybir.dt.float32
+BF16 = mybir.dt.bfloat16
+I32 = mybir.dt.int32
+U32 = mybir.dt.uint32
+U16 = mybir.dt.uint16
+U8 = mybir.dt.uint8
+FP8X4 = mybir.dt.float8_e4m3fn_x4
+ALU = mybir.AluOpType
+COPY = mybir.ActivationFunctionType.Copy
+
+P = 128
+PACK = 4
+GATHER_W = S + 16
+SCATTER_W = S + 128
+HALF = S // 2
+
+
+def tile_picked_mhhzqsndminpags_none_p_kernel(tc, x_words, x_scales, d_words, d_scales, gs, offs, k1, hz, k2, n1, n2, n3, k3, n4, n5, out):
+    nc = tc.nc
+    with ExitStack() as ctx:
+        lists = ctx.enter_context(tc.tile_pool(name="lists", bufs=1))
+        keep = ctx.enter_context(tc.tile_pool(name="keep", bufs=1))
+        psum = ctx.enter_context(tc.psum_pool(name="psum", bufs=1))
+
+        def load_list(src, name):
+            tile = lists.tile([P, src.shape[1]], U16, name=name)
+            nc.sync.dma_start(tile[:], src)
+            return tile
+
+        def place_scale_rows(plane, gathered):
+            for q in range(4):
+                nc.sync.dma_start(plane[32 * q : 32 * q + 4, :].bitcast(I32), gathered[32 * q : 32 * q + 32 : 8, :].bitcast(I32))
+
+        d_byte_tab = keep.tile([P, G], U8, align_bytes=64)
+        x_byte_tab = keep.tile([P, T], U8, align_bytes=64)
+        nc.sync.dma_start(d_byte_tab[:].bitcast(I32), d_scales[0].bitcast(I32).unsqueeze(1).to_broadcast([16, 8, G // 4]))
+        k1_l = load_list(k1, "k1_l")
+        k2_l = load_list(k2, "k2_l")
+        nc.sync.dma_start(x_byte_tab[:].bitcast(I32), x_scales[0].bitcast(I32).unsqueeze(1).to_broadcast([16, 8, T // 4]))
+        offs_l = load_list(offs, "offs_l")
+        hz_l = load_list(hz, "hz_l")
+        d_word_tab = keep.tile([P, G], U32, align_bytes=64)
+        x_word_tab = keep.tile([P, T], U32, align_bytes=64)
+        nc.sync.dma_start(d_word_tab[:].bitcast(I32), d_words[0].rearrange("p n t -> p (n t)").bitcast(I32))
+        nc.sync.dma_start(x_word_tab[:].bitcast(I32), x_words[0].rearrange("p n t -> p (n t)").bitcast(I32))
+        n1_l = load_list(n1, "n1_l")
+        n2_l = load_list(n2, "n2_l")
+        n3_l = load_list(n3, "n3_l")
+        k3_l = load_list(k3, "k3_l")
+        n5_l = load_list(n5, "n5_l")
+        n4_l = load_list(n4, "n4_l")
+        gain = keep.tile([P, PACK], F32)
+        nc.gpsimd.dma_start(gain[:], gs.rearrange("(p t) o -> p (t o)", t=PACK))
+        neg_gain = keep.tile([P, PACK], F32)
+        nc.gpsimd.tensor_scalar(neg_gain[:], gain[:], -1.0, 0.0, ALU.mult, ALU.add)
+
+        plane1 = keep.tile([P, 2 * H + 2 * S], U8, align_bytes=64)
+        plane3 = keep.tile([P, H], U8, align_bytes=64)
+        nc.vector.memset(plane1[:].bitcast(I32), 0)
+        nc.vector.memset(plane3[:].bitcast(I32), 0)
+
+        pages = [keep.tile([P, U], F32, name="page%d" % t) for t in range(PACK)]
+        nc.vector.memset(pages[0][:], 0.0)
+        for t in range(1, PACK):
+            nc.scalar.copy(pages[t][:], pages[0][:])
+
+        h = [keep.tile([P, GATHER_W], F32, name="h%d" % t) for t in range(PACK)]
+        st = [keep.tile([P, GATHER_W], F32, name="st%d" % t) for t in range(PACK)]
+        h2 = [keep.tile([P, GATHER_W], F32, name="h2%d" % t) for t in range(PACK)]
+        for tile in h + st + h2:
+            nc.gpsimd.memset(tile[:, S:], 0.0)
+
+        d_bytes = keep.tile([P, 2 * H], U8, align_bytes=64, tag="d_gathered")
+        x_bytes = keep.tile([P, 2 * S], U8, align_bytes=64, tag="x_gathered")
+        nc.vector.tensor_copy(d_bytes[:, :H], d_byte_tab[:].indirect(k1_l[:]))
+        nc.vector.tensor_copy(d_bytes[:, H:], d_byte_tab[:].indirect(k2_l[:]))
+        nc.vector.tensor_copy(x_bytes[:, :S], x_byte_tab[:].indirect(offs_l[:]))
+        nc.vector.tensor_copy(x_bytes[:, S:], x_byte_tab[:].indirect(hz_l[:]))
+        dealt_bytes = keep.tile([P, 2 * H + 2 * S], U8, align_bytes=64)
+        nc.vector.tensor_copy(
+            dealt_bytes[:, : 2 * H].rearrange("p (l t m) -> p l t m", l=2, t=PACK),
+            d_bytes[:].rearrange("p (l m t) -> p l t m", l=2, t=PACK),
+        )
+        nc.vector.tensor_copy(dealt_bytes[:, 2 * H :].bitcast(I32), x_bytes[:].bitcast(I32))
+        place_scale_rows(plane1, dealt_bytes)
+
+        d_picked = keep.tile([P, 2 * H], U32, align_bytes=64, tag="d_gathered")
+        x_picked = keep.tile([P, 2 * S], U32, align_bytes=64, tag="x_gathered")
+        xq, xh = x_picked[:, :S], x_picked[:, S:]
+        nc.vector.tensor_copy(d_picked[:, :H], d_word_tab[:].indirect(k1_l[:]))
+        nc.vector.tensor_copy(d_picked[:, H:], d_word_tab[:].indirect(k2_l[:]))
+        nc.vector.tensor_copy(xq, x_word_tab[:].indirect(offs_l[:]))
+        d_view = d_picked[:].rearrange("p (l m t) -> p l m t", l=2, t=PACK)
+        dealt_first = keep.tile([P, 2, P], U32, align_bytes=64)
+        dealt_rest = keep.tile([P, PACK - 1, 2, P], U32, align_bytes=64)
+        nc.vector.tensor_copy(dealt_first[:], d_view[:, :, :, 0])
+        nc.vector.tensor_copy(xh, x_word_tab[:].indirect(hz_l[:]))
+        nc.vector.tensor_copy(dealt_rest[:].rearrange("p t l m -> p l m t"), d_view[:, :, :, 1:])
+
+        banks = [psum.tile([P, S], F32, name="bank%d" % t, tag="bank%d" % t) for t in range(PACK)]
+        for t in range(PACK):
+            for l, moving in enumerate((xq, xh)):
+                stationary = dealt_first[:, l, :] if t == 0 else dealt_rest[:, t - 1, l, :]
+                nc.tensor.matmul_mx(
+                    out=banks[t][:],
+                    lhsT=stationary.bitcast(FP8X4),
+                    lhsT_scale=plane1[:, l * H + t * P : l * H + (t + 1) * P],
+                    rhs=moving.bitcast(FP8X4),
+                    rhs_scale=plane1[:, 2 * H + l * S : 2 * H + (l + 1) * S],
+                    start=(l == 0),
+                    stop=(l == 1),
+                )
+        nc.scalar.activation(h[0][:, :S], banks[0][:], COPY, scale=0.0625)
+        for t in range(1, PACK):
+            nc.vector.tensor_scalar(h[t][:, :S], banks[t][:], 0.0625, None, ALU.mult)
+
+        ds = [keep.tile([P, SCATTER_W], F32, name="ds%d" % t) for t in range(PACK)]
+        hg = [keep.tile([P, S], F32, name="hg%d" % t) for t in range(PACK)]
+        sg = [keep.tile([P, S], F32, name="sg%d" % t) for t in range(PACK)]
+        stg = [keep.tile([P, S], F32, name="stg%d" % t) for t in range(PACK)]
+        z = keep.tile([P, S, PACK], BF16, align_bytes=64)
+
+        def step_one(t):
+            nc.scalar.activation(ds[t][:].indirect(n1_l[:]), h[t][:, :S], COPY)
+            nc.scalar.activation(hg[t][:], h[t][:].indirect(n2_l[:]), COPY)
+            nc.vector.tensor_tensor(st[t][:, :S], ds[t][:, :S], hg[t][:], ALU.min)
+            nc.vector.tensor_scalar(sg[t][:], st[t][:, :S], gain[:, t : t + 1], None, ALU.mult)
+
+        def step_two(t, lo, hi):
+            nc.scalar.activation(stg[t][:, lo:hi], st[t][:].indirect(n3_l[:, lo // 16 : hi // 16]), COPY)
+            nc.vector.scalar_tensor_tensor(z[:, lo:hi, t], stg[t][:, lo:hi], neg_gain[:, t : t + 1], sg[t][:, lo:hi], ALU.mult, ALU.add)
+
+        step_one(0)
+        d3_bytes = keep.tile([P, H], U8, align_bytes=64, tag="x_gathered")
+        d3_words = keep.tile([P, H], U32, align_bytes=64, tag="d_gathered")
+        for c in range(2):
+            nc.vector.tensor_copy(d3_bytes[:, c * S : (c + 1) * S], d_byte_tab[:].indirect(k3_l[:, c * 16 : (c + 1) * 16]))
+        place_scale_rows(plane3, d3_bytes)
+        for c in range(2):
+            nc.vector.tensor_copy(d3_words[:, c * S : (c + 1) * S], d_word_tab[:].indirect(k3_l[:, c * 16 : (c + 1) * 16]))
+        for t in range(1, PACK):
+            step_one(t)
+            step_two(t - 1, 0, S)
+        z_words = keep.tile([P, S], U32, align_bytes=64)
+        z_plane = keep.tile([P, S], U8, align_bytes=64)
+        for c in range(2):
+            cols = slice(c * HALF, (c + 1) * HALF)
+            step_two(PACK - 1, cols.start, cols.stop)
+            nc.vector.quantize_mx(out=z_words[:, cols].bitcast(FP8X4), scales=z_plane[:, cols], in_=z[:, cols, :].rearrange("p j t -> p (j t)"))
+            for t in range(PACK):
+                tag = "bank%d" % (t + PACK * (1 - c))
+                acc = psum.tile([P, S], F32, name="acc", tag=tag)
+                nc.tensor.matmul_mx(
+                    out=acc[:, :HALF],
+                    lhsT=d3_words[:, t * P : (t + 1) * P].bitcast(FP8X4),
+                    lhsT_scale=plane3[:, t * P : (t + 1) * P],
+                    rhs=z_words[:, cols].bitcast(FP8X4),
+                    rhs_scale=z_plane[:, cols],
+                    start=True,
+                    stop=True,
+                )
+                if t == 0:
+                    nc.scalar.activation(h2[t][:, cols], acc[:, :HALF], COPY, scale=0.0625)
+                else:
+                    nc.vector.tensor_scalar(h2[t][:, cols], acc[:, :HALF], 0.0625, None, ALU.mult)
+
+        h2g = [keep.tile([P, S], F32, name="h2g%d" % t) for t in range(PACK)]
+        nw = [keep.tile([P, S], F32, name="nw%d" % t) for t in range(PACK)]
+
+        def fetch(t):
+            nc.scalar.activation(h2g[t][:], h2[t][:].indirect(n5_l[:]), COPY)
+            nc.vector.tensor_tensor(nw[t][:], h2[t][:, :S], h2g[t][:], ALU.max)
+
+        def put(t):
+            nc.scalar.activation(pages[t][:].indirect(n4_l[:]), nw[t][:], COPY)
+            nc.sync.dma_start(out[t * P : (t + 1) * P, :], pages[t][:])
+
+        fetch(0)
+        for t in range(1, PACK):
+            fetch(t)
+            put(t - 1)
+        put(PACK - 1)

@@ -1,6 +1,7 @@
 from contextlib import ExitStack
 
 import concourse.mybir as mybir
+from concourse.masks import make_identity
 
 K, T, S, G, H, U = 512, 1024, 256, 2048, 512, 1024
 FLOPS = 3 * 2 * K * H * S
@@ -17,9 +18,11 @@ COPY = mybir.ActivationFunctionType.Copy
 
 P = 128
 PACK = 4
+TILES = H // P
 GATHER_W = S + 16
 SCATTER_W = S + 128
 HALF = S // 2
+PIECE = H // 2
 
 
 def tile_picked_mhhzqsndminpags_none_p_kernel(tc, x_words, x_scales, d_words, d_scales, gs, offs, k1, hz, k2, n1, n2, n3, k3, n4, n5, out):
@@ -38,141 +41,188 @@ def tile_picked_mhhzqsndminpags_none_p_kernel(tc, x_words, x_scales, d_words, d_
             for q in range(4):
                 nc.sync.dma_start(plane[32 * q : 32 * q + 4, :].bitcast(I32), gathered[32 * q : 32 * q + 32 : 8, :].bitcast(I32))
 
+        def bank(number, shape):
+            return psum.tile(shape, F32, name="bank", tag="bank%d" % number)
+
         d_byte_tab = keep.tile([P, G], U8, align_bytes=64)
         x_byte_tab = keep.tile([P, T], U8, align_bytes=64)
-        nc.sync.dma_start(d_byte_tab[:].bitcast(I32), d_scales[0].bitcast(I32).unsqueeze(1).to_broadcast([16, 8, G // 4]))
-        k1_l = load_list(k1, "k1_l")
-        k2_l = load_list(k2, "k2_l")
         nc.sync.dma_start(x_byte_tab[:].bitcast(I32), x_scales[0].bitcast(I32).unsqueeze(1).to_broadcast([16, 8, T // 4]))
         offs_l = load_list(offs, "offs_l")
         hz_l = load_list(hz, "hz_l")
+        nc.sync.dma_start(d_byte_tab[:].bitcast(I32), d_scales[0].bitcast(I32).unsqueeze(1).to_broadcast([16, 8, G // 4]))
+        k1_l = load_list(k1, "k1_l")
+        k2_l = load_list(k2, "k2_l")
         d_word_tab = keep.tile([P, G], U32, align_bytes=64)
         x_word_tab = keep.tile([P, T], U32, align_bytes=64)
         nc.sync.dma_start(d_word_tab[:].bitcast(I32), d_words[0].rearrange("p n t -> p (n t)").bitcast(I32))
-        nc.sync.dma_start(x_word_tab[:].bitcast(I32), x_words[0].rearrange("p n t -> p (n t)").bitcast(I32))
         n1_l = load_list(n1, "n1_l")
         n2_l = load_list(n2, "n2_l")
         n3_l = load_list(n3, "n3_l")
         k3_l = load_list(k3, "k3_l")
+        nc.sync.dma_start(x_word_tab[:].bitcast(I32), x_words[0].rearrange("p n t -> p (n t)").bitcast(I32))
         n5_l = load_list(n5, "n5_l")
         n4_l = load_list(n4, "n4_l")
         gain = keep.tile([P, PACK], F32)
-        nc.gpsimd.dma_start(gain[:], gs.rearrange("(p t) o -> p (t o)", t=PACK))
-        neg_gain = keep.tile([P, PACK], F32)
-        nc.gpsimd.tensor_scalar(neg_gain[:], gain[:], -1.0, 0.0, ALU.mult, ALU.add)
+        nc.sync.dma_start(gain[:], gs.rearrange("(p s) o -> p (s o)", s=PACK))
 
-        plane1 = keep.tile([P, 2 * H + 2 * S], U8, align_bytes=64)
-        plane3 = keep.tile([P, H], U8, align_bytes=64)
-        nc.vector.memset(plane1[:].bitcast(I32), 0)
-        nc.vector.memset(plane3[:].bitcast(I32), 0)
+        plane_a = keep.tile([P, 2 * S + 2 * PIECE], U8, align_bytes=64)
+        plane_b = keep.tile([P, 2 * PIECE], U8, align_bytes=64)
+        plane_3 = keep.tile([P, H], U8, align_bytes=64)
+        for plane in (plane_a, plane_b, plane_3):
+            nc.vector.memset(plane[:].bitcast(I32), 0)
 
-        pages = [keep.tile([P, U], F32, name="page%d" % t) for t in range(PACK)]
+        pages = [keep.tile([P, U], F32, name="page%d" % t) for t in range(TILES)]
         nc.vector.memset(pages[0][:], 0.0)
-        for t in range(1, PACK):
+        for t in range(1, TILES):
             nc.scalar.copy(pages[t][:], pages[0][:])
 
-        h = [keep.tile([P, GATHER_W], F32, name="h%d" % t) for t in range(PACK)]
-        st = [keep.tile([P, GATHER_W], F32, name="st%d" % t) for t in range(PACK)]
-        h2 = [keep.tile([P, GATHER_W], F32, name="h2%d" % t) for t in range(PACK)]
+        ident = keep.tile([P, P], F32)
+        make_identity(nc, ident[:])
+        h = [keep.tile([P, GATHER_W], F32, name="h%d" % t) for t in range(TILES)]
+        st = [keep.tile([P, GATHER_W], F32, name="st%d" % t) for t in range(TILES)]
+        h2 = [keep.tile([P, GATHER_W], F32, name="h2%d" % t) for t in range(TILES)]
         for tile in h + st + h2:
             nc.gpsimd.memset(tile[:, S:], 0.0)
 
-        d_bytes = keep.tile([P, 2 * H], U8, align_bytes=64, tag="d_gathered")
-        x_bytes = keep.tile([P, 2 * S], U8, align_bytes=64, tag="x_gathered")
-        nc.vector.tensor_copy(d_bytes[:, :H], d_byte_tab[:].indirect(k1_l[:]))
-        nc.vector.tensor_copy(d_bytes[:, H:], d_byte_tab[:].indirect(k2_l[:]))
-        nc.vector.tensor_copy(x_bytes[:, :S], x_byte_tab[:].indirect(offs_l[:]))
-        nc.vector.tensor_copy(x_bytes[:, S:], x_byte_tab[:].indirect(hz_l[:]))
-        dealt_bytes = keep.tile([P, 2 * H + 2 * S], U8, align_bytes=64)
-        nc.vector.tensor_copy(
-            dealt_bytes[:, : 2 * H].rearrange("p (l t m) -> p l t m", l=2, t=PACK),
-            d_bytes[:].rearrange("p (l m t) -> p l t m", l=2, t=PACK),
-        )
-        nc.vector.tensor_copy(dealt_bytes[:, 2 * H :].bitcast(I32), x_bytes[:].bitcast(I32))
-        place_scale_rows(plane1, dealt_bytes)
+        def piece(tile, c):
+            return tile[:, c * PIECE // 16 : (c + 1) * PIECE // 16]
 
-        d_picked = keep.tile([P, 2 * H], U32, align_bytes=64, tag="d_gathered")
-        x_picked = keep.tile([P, 2 * S], U32, align_bytes=64, tag="x_gathered")
-        xq, xh = x_picked[:, :S], x_picked[:, S:]
-        nc.vector.tensor_copy(d_picked[:, :H], d_word_tab[:].indirect(k1_l[:]))
-        nc.vector.tensor_copy(d_picked[:, H:], d_word_tab[:].indirect(k2_l[:]))
-        nc.vector.tensor_copy(xq, x_word_tab[:].indirect(offs_l[:]))
-        d_view = d_picked[:].rearrange("p (l m t) -> p l m t", l=2, t=PACK)
-        dealt_first = keep.tile([P, 2, P], U32, align_bytes=64)
-        dealt_rest = keep.tile([P, PACK - 1, 2, P], U32, align_bytes=64)
-        nc.vector.tensor_copy(dealt_first[:], d_view[:, :, :, 0])
-        nc.vector.tensor_copy(xh, x_word_tab[:].indirect(hz_l[:]))
-        nc.vector.tensor_copy(dealt_rest[:].rearrange("p t l m -> p l m t"), d_view[:, :, :, 1:])
+        bytes_a = keep.tile([P, 2 * S + 2 * PIECE], U8, align_bytes=64, tag="picked_bytes")
+        nc.vector.tensor_copy(bytes_a[:, :S], x_byte_tab[:].indirect(offs_l[:]))
+        nc.vector.tensor_copy(bytes_a[:, S : 2 * S], x_byte_tab[:].indirect(hz_l[:]))
+        nc.vector.tensor_copy(bytes_a[:, 2 * S : 2 * S + PIECE], d_byte_tab[:].indirect(piece(k1_l, 0)))
+        nc.vector.tensor_copy(bytes_a[:, 2 * S + PIECE :], d_byte_tab[:].indirect(piece(k2_l, 0)))
+        place_scale_rows(plane_a, bytes_a)
 
-        banks = [psum.tile([P, S], F32, name="bank%d" % t, tag="bank%d" % t) for t in range(PACK)]
-        for t in range(PACK):
-            for l, moving in enumerate((xq, xh)):
-                stationary = dealt_first[:, l, :] if t == 0 else dealt_rest[:, t - 1, l, :]
+        x_picked = keep.tile([P, 2 * S], U32, align_bytes=64, tag="words_x")
+        words_a = keep.tile([P, 2 * PIECE], U32, align_bytes=64, tag="words_d")
+        nc.vector.tensor_copy(words_a[:, :PIECE], d_word_tab[:].indirect(piece(k1_l, 0)))
+        nc.vector.tensor_copy(words_a[:, PIECE:], d_word_tab[:].indirect(piece(k2_l, 0)))
+        nc.vector.tensor_copy(x_picked[:, :S], x_word_tab[:].indirect(offs_l[:]))
+        nc.vector.tensor_copy(x_picked[:, S:], x_word_tab[:].indirect(hz_l[:]))
+
+        def first_products(t, words, scales):
+            acc = bank(t, [P, S])
+            for l in range(2):
+                cols = slice(l * PIECE + (t % 2) * P, l * PIECE + (t % 2 + 1) * P)
                 nc.tensor.matmul_mx(
-                    out=banks[t][:],
-                    lhsT=stationary.bitcast(FP8X4),
-                    lhsT_scale=plane1[:, l * H + t * P : l * H + (t + 1) * P],
-                    rhs=moving.bitcast(FP8X4),
-                    rhs_scale=plane1[:, 2 * H + l * S : 2 * H + (l + 1) * S],
+                    out=acc[:],
+                    lhsT=words[:, cols].bitcast(FP8X4),
+                    lhsT_scale=scales[:, cols],
+                    rhs=x_picked[:, l * S : (l + 1) * S].bitcast(FP8X4),
+                    rhs_scale=plane_a[:, l * S : (l + 1) * S],
                     start=(l == 0),
                     stop=(l == 1),
                 )
-        nc.scalar.activation(h[0][:, :S], banks[0][:], COPY, scale=0.0625)
-        for t in range(1, PACK):
-            nc.vector.tensor_scalar(h[t][:, :S], banks[t][:], 0.0625, None, ALU.mult)
+            if t == 0:
+                nc.scalar.activation(h[t][:, :S], acc[:], COPY, scale=0.0625)
+            else:
+                nc.vector.tensor_scalar(h[t][:, :S], acc[:], 0.0625, None, ALU.mult)
 
-        ds = [keep.tile([P, SCATTER_W], F32, name="ds%d" % t) for t in range(PACK)]
-        hg = [keep.tile([P, S], F32, name="hg%d" % t) for t in range(PACK)]
-        sg = [keep.tile([P, S], F32, name="sg%d" % t) for t in range(PACK)]
-        stg = [keep.tile([P, S], F32, name="stg%d" % t) for t in range(PACK)]
-        z = keep.tile([P, S, PACK], BF16, align_bytes=64)
+        first_products(0, words_a, plane_a[:, 2 * S :])
+        bytes_b = keep.tile([P, 2 * PIECE], U8, align_bytes=64, tag="picked_bytes")
+        nc.vector.tensor_copy(bytes_b[:, :PIECE], d_byte_tab[:].indirect(piece(k1_l, 1)))
+        nc.vector.tensor_copy(bytes_b[:, PIECE:], d_byte_tab[:].indirect(piece(k2_l, 1)))
+        place_scale_rows(plane_b, bytes_b)
+        first_products(1, words_a, plane_a[:, 2 * S :])
+        words_b = keep.tile([P, 2 * PIECE], U32, align_bytes=64, tag="words_d")
+        nc.vector.tensor_copy(words_b[:, :PIECE], d_word_tab[:].indirect(piece(k1_l, 1)))
+        nc.vector.tensor_copy(words_b[:, PIECE:], d_word_tab[:].indirect(piece(k2_l, 1)))
+
+        gain_bank = bank(1, [P, PACK, P])
+        for s in range(PACK):
+            nc.tensor.transpose(gain_bank[:, s, :], gain[:, s : s + 1].to_broadcast([P, P]), ident[:])
+        gain_row = keep.tile([P, TILES, 2, 32, 2], F32)
+        nc.vector.tensor_copy(gain_row[:], gain_bank[:].rearrange("m (u e) (t q) -> m t u q e", u=2, t=TILES))
+
+        ds = [keep.tile([P, SCATTER_W], F32, name="ds%d" % t) for t in range(TILES)]
+        hg = [keep.tile([P, S], F32, name="hg%d" % t) for t in range(TILES)]
+        neg_stg = [keep.tile([P, S], F32, name="neg_stg%d" % t) for t in range(TILES)]
+        z_turned = [keep.tile([P, 2, 2 * P], BF16, name="z_turned%d" % c) for c in range(2)]
+        diff = {}
 
         def step_one(t):
             nc.scalar.activation(ds[t][:].indirect(n1_l[:]), h[t][:, :S], COPY)
             nc.scalar.activation(hg[t][:], h[t][:].indirect(n2_l[:]), COPY)
             nc.vector.tensor_tensor(st[t][:, :S], ds[t][:, :S], hg[t][:], ALU.min)
-            nc.vector.tensor_scalar(sg[t][:], st[t][:, :S], gain[:, t : t + 1], None, ALU.mult)
 
-        def step_two(t, lo, hi):
-            nc.scalar.activation(stg[t][:, lo:hi], st[t][:].indirect(n3_l[:, lo // 16 : hi // 16]), COPY)
-            nc.vector.scalar_tensor_tensor(z[:, lo:hi, t], stg[t][:, lo:hi], neg_gain[:, t : t + 1], sg[t][:, lo:hi], ALU.mult, ALU.add)
+        def fetch_st(t, lo, hi):
+            nc.scalar.activation(neg_stg[t][:, lo:hi], st[t][:].indirect(n3_l[:, lo // 16 : hi // 16]), COPY, scale=-1.0)
+
+        def turn_st(t, c):
+            diff[t, c] = bank((2, 2, 0, 4)[t] + c, [P, P])
+            nc.tensor.matmul(diff[t, c][:], st[t][:, c * HALF : (c + 1) * HALF], ident[:], start=True, stop=False, is_transpose=True)
+
+        def turn_diff(t, c):
+            nc.tensor.matmul(diff[t, c][:], neg_stg[t][:, c * HALF : (c + 1) * HALF], ident[:], start=False, stop=True, is_transpose=True)
+            nc.vector.tensor_tensor(
+                z_turned[c][:, :, 64 * t : 64 * (t + 1)].rearrange("j u (q e) -> j u q e", e=2),
+                diff[t, c][:].rearrange("j (q u e) -> j u q e", u=2, e=2),
+                gain_row[:, t],
+                ALU.mult,
+            )
+
+        def step_two(t):
+            fetch_st(t, 0, S)
+            for c in range(2):
+                turn_st(t, c)
+            for c in range(2):
+                turn_diff(t, c)
 
         step_one(0)
-        d3_bytes = keep.tile([P, H], U8, align_bytes=64, tag="x_gathered")
-        d3_words = keep.tile([P, H], U32, align_bytes=64, tag="d_gathered")
+        step_one(1)
+        first_products(2, words_b, plane_b)
+        first_products(3, words_b, plane_b)
+        d3_bytes = keep.tile([P, H], U8, align_bytes=64, tag="words_d")
+        d3_words = keep.tile([P, H], U32, align_bytes=64, tag="words_x")
+        step_two(0)
         for c in range(2):
-            nc.vector.tensor_copy(d3_bytes[:, c * S : (c + 1) * S], d_byte_tab[:].indirect(k3_l[:, c * 16 : (c + 1) * 16]))
-        place_scale_rows(plane3, d3_bytes)
+            nc.vector.tensor_copy(d3_bytes[:, c * PIECE : (c + 1) * PIECE], d_byte_tab[:].indirect(piece(k3_l, c)))
+        place_scale_rows(plane_3, d3_bytes)
+        step_one(2)
+        step_two(1)
         for c in range(2):
-            nc.vector.tensor_copy(d3_words[:, c * S : (c + 1) * S], d_word_tab[:].indirect(k3_l[:, c * 16 : (c + 1) * 16]))
-        for t in range(1, PACK):
-            step_one(t)
-            step_two(t - 1, 0, S)
+            nc.vector.tensor_copy(d3_words[:, c * PIECE : (c + 1) * PIECE], d_word_tab[:].indirect(piece(k3_l, c)))
+        step_one(3)
+        step_two(2)
+
+        last = TILES - 1
+        for c in range(2):
+            turn_st(last, c)
+        for c in range(2):
+            fetch_st(last, c * HALF, (c + 1) * HALF)
+            turn_diff(last, c)
         z_words = keep.tile([P, S], U32, align_bytes=64)
         z_plane = keep.tile([P, S], U8, align_bytes=64)
+        z = [keep.tile([P, PACK * HALF], BF16, align_bytes=64, name="z%d" % c) for c in range(2)]
         for c in range(2):
-            cols = slice(c * HALF, (c + 1) * HALF)
-            step_two(PACK - 1, cols.start, cols.stop)
-            nc.vector.quantize_mx(out=z_words[:, cols].bitcast(FP8X4), scales=z_plane[:, cols], in_=z[:, cols, :].rearrange("p j t -> p (j t)"))
-            for t in range(PACK):
-                tag = "bank%d" % (t + PACK * (1 - c))
-                acc = psum.tile([P, S], F32, name="acc", tag=tag)
-                nc.tensor.matmul_mx(
-                    out=acc[:, :HALF],
-                    lhsT=d3_words[:, t * P : (t + 1) * P].bitcast(FP8X4),
-                    lhsT_scale=plane3[:, t * P : (t + 1) * P],
-                    rhs=z_words[:, cols].bitcast(FP8X4),
-                    rhs_scale=z_plane[:, cols],
-                    start=True,
-                    stop=True,
-                )
-                if t == 0:
-                    nc.scalar.activation(h2[t][:, cols], acc[:, :HALF], COPY, scale=0.0625)
-                else:
-                    nc.vector.tensor_scalar(h2[t][:, cols], acc[:, :HALF], 0.0625, None, ALU.mult)
+            back = bank(6 + c, [P, 2, HALF])
+            pairs = z_turned[c][:].bitcast(F32)
+            for u in range(2):
+                nc.tensor.transpose(back[:, u, :], pairs[:, u, :], ident[:])
+            nc.scalar.copy(z[c][:].bitcast(F32).rearrange("p (j u) -> p j u", u=2), back[:].rearrange("p u j -> p j u"))
+        def last_product(t, cols, number):
+            acc = bank(number, [P, cols.stop - cols.start])
+            nc.tensor.matmul_mx(
+                out=acc[:],
+                lhsT=d3_words[:, t * P : (t + 1) * P].bitcast(FP8X4),
+                lhsT_scale=plane_3[:, t * P : (t + 1) * P],
+                rhs=z_words[:, cols].bitcast(FP8X4),
+                rhs_scale=z_plane[:, cols],
+                start=True,
+                stop=True,
+            )
+            nc.vector.tensor_scalar(h2[t][:, cols], acc[:], 0.0625, None, ALU.mult)
 
-        h2g = [keep.tile([P, S], F32, name="h2g%d" % t) for t in range(PACK)]
-        nw = [keep.tile([P, S], F32, name="nw%d" % t) for t in range(PACK)]
+        for c in range(2):
+            nc.vector.quantize_mx(out=z_words[:, c * HALF : (c + 1) * HALF].bitcast(FP8X4), scales=z_plane[:, c * HALF : (c + 1) * HALF], in_=z[c][:])
+        for c in range(2):
+            last_product(0, slice(c * HALF, (c + 1) * HALF), c)
+        for t in range(1, TILES):
+            last_product(t, slice(0, S), 1 + t)
+
+        h2g = [keep.tile([P, S], F32, name="h2g%d" % t) for t in range(TILES)]
+        nw = [keep.tile([P, S], F32, name="nw%d" % t) for t in range(TILES)]
 
         def fetch(t):
             nc.scalar.activation(h2g[t][:], h2[t][:].indirect(n5_l[:]), COPY)
@@ -183,7 +233,7 @@ def tile_picked_mhhzqsndminpags_none_p_kernel(tc, x_words, x_scales, d_words, d_
             nc.sync.dma_start(out[t * P : (t + 1) * P, :], pages[t][:])
 
         fetch(0)
-        for t in range(1, PACK):
+        for t in range(1, TILES):
             fetch(t)
             put(t - 1)
-        put(PACK - 1)
+        put(TILES - 1)

@@ -87,47 +87,59 @@ def tile_picked_mhhzqsndminpags_none_p_kernel(tc, x_words, x_scales, d_words, d_
         def piece(tile, c):
             return tile[:, c * PIECE // 16 : (c + 1) * PIECE // 16]
 
-        bytes_a = keep.tile([P, 2 * S + 2 * PIECE], U8, align_bytes=64, tag="picked_bytes")
+        def half(tile, c):
+            return tile[:, c * HALF // 16 : (c + 1) * HALF // 16]
+
+        bytes_a = keep.tile([P, 2 * S + 2 * PIECE], U8, align_bytes=64)
         nc.vector.tensor_copy(bytes_a[:, :S], x_byte_tab[:].indirect(offs_l[:]))
         nc.vector.tensor_copy(bytes_a[:, S : 2 * S], x_byte_tab[:].indirect(hz_l[:]))
         nc.vector.tensor_copy(bytes_a[:, 2 * S : 2 * S + PIECE], d_byte_tab[:].indirect(piece(k1_l, 0)))
         nc.vector.tensor_copy(bytes_a[:, 2 * S + PIECE :], d_byte_tab[:].indirect(piece(k2_l, 0)))
         place_scale_rows(plane_a, bytes_a)
 
-        x_picked = keep.tile([P, 2 * S], U32, align_bytes=64, tag="words_x")
-        words_a = keep.tile([P, 2 * PIECE], U32, align_bytes=64, tag="words_d")
-        nc.vector.tensor_copy(words_a[:, :PIECE], d_word_tab[:].indirect(piece(k1_l, 0)))
-        nc.vector.tensor_copy(words_a[:, PIECE:], d_word_tab[:].indirect(piece(k2_l, 0)))
-        nc.vector.tensor_copy(x_picked[:, :S], x_word_tab[:].indirect(offs_l[:]))
-        nc.vector.tensor_copy(x_picked[:, S:], x_word_tab[:].indirect(hz_l[:]))
+        x_picked = [keep.tile([P, 2 * HALF], U32, align_bytes=64, name="x_picked", tag="words_x%d" % c) for c in range(2)]
+        words_a = [keep.tile([P, PIECE], U32, align_bytes=64, name="words_a", tag="words_d%d" % l) for l in range(2)]
+        nc.vector.tensor_copy(words_a[0][:], d_word_tab[:].indirect(piece(k1_l, 0)))
+        nc.vector.tensor_copy(words_a[1][:], d_word_tab[:].indirect(piece(k2_l, 0)))
+        for c in range(2):
+            nc.vector.tensor_copy(x_picked[c][:, :HALF], x_word_tab[:].indirect(half(offs_l, c)))
+            nc.vector.tensor_copy(x_picked[c][:, HALF:], x_word_tab[:].indirect(half(hz_l, c)))
 
-        def first_products(t, words, scales):
-            acc = bank(t, [P, S])
+        def first_products(t, c, acc, words, scales):
             for l in range(2):
-                cols = slice(l * PIECE + (t % 2) * P, l * PIECE + (t % 2 + 1) * P)
                 nc.tensor.matmul_mx(
-                    out=acc[:],
-                    lhsT=words[:, cols].bitcast(FP8X4),
-                    lhsT_scale=scales[:, cols],
-                    rhs=x_picked[:, l * S : (l + 1) * S].bitcast(FP8X4),
-                    rhs_scale=plane_a[:, l * S : (l + 1) * S],
+                    out=acc,
+                    lhsT=words[l][:, (t % 2) * P : (t % 2 + 1) * P].bitcast(FP8X4),
+                    lhsT_scale=scales[:, l * PIECE + (t % 2) * P : l * PIECE + (t % 2 + 1) * P],
+                    rhs=x_picked[c][:, l * HALF : (l + 1) * HALF].bitcast(FP8X4),
+                    rhs_scale=plane_a[:, l * S + c * HALF : l * S + (c + 1) * HALF],
                     start=(l == 0),
                     stop=(l == 1),
                 )
-            if t == 0:
-                nc.scalar.activation(h[t][:, :S], acc[:], COPY, scale=0.0625)
-            else:
-                nc.vector.tensor_scalar(h[t][:, :S], acc[:], 0.0625, None, ALU.mult)
 
-        first_products(0, words_a, plane_a[:, 2 * S :])
-        bytes_b = keep.tile([P, 2 * PIECE], U8, align_bytes=64, tag="picked_bytes")
+        for c in range(2):
+            for t in range(2):
+                acc = bank(4 * c + t, [P, HALF])
+                first_products(t, c, acc[:], words_a, plane_a[:, 2 * S :])
+                if t == 0 and c == 0:
+                    nc.scalar.activation(h[t][:, :HALF], acc[:], COPY, scale=0.0625)
+                else:
+                    nc.vector.tensor_scalar(h[t][:, c * HALF : (c + 1) * HALF], acc[:], 0.0625, None, ALU.mult)
+
+        def late_products(t):
+            acc = bank(t, [P, S])
+            for c in range(2):
+                first_products(t, c, acc[:, c * HALF : (c + 1) * HALF], words_b, plane_b)
+            nc.vector.tensor_scalar(h[t][:, :S], acc[:], 0.0625, None, ALU.mult)
+
+        bytes_b = keep.tile([P, 2 * PIECE], U8, align_bytes=64, tag="words_d0")
         nc.vector.tensor_copy(bytes_b[:, :PIECE], d_byte_tab[:].indirect(piece(k1_l, 1)))
         nc.vector.tensor_copy(bytes_b[:, PIECE:], d_byte_tab[:].indirect(piece(k2_l, 1)))
         place_scale_rows(plane_b, bytes_b)
-        first_products(1, words_a, plane_a[:, 2 * S :])
-        words_b = keep.tile([P, 2 * PIECE], U32, align_bytes=64, tag="words_d")
-        nc.vector.tensor_copy(words_b[:, :PIECE], d_word_tab[:].indirect(piece(k1_l, 1)))
-        nc.vector.tensor_copy(words_b[:, PIECE:], d_word_tab[:].indirect(piece(k2_l, 1)))
+        both_b = keep.tile([P, 2 * PIECE], U32, align_bytes=64, tag="words_d1")
+        words_b = [both_b[:, :PIECE], both_b[:, PIECE:]]
+        nc.vector.tensor_copy(words_b[0], d_word_tab[:].indirect(piece(k1_l, 1)))
+        nc.vector.tensor_copy(words_b[1], d_word_tab[:].indirect(piece(k2_l, 1)))
 
         gain_bank = bank(1, [P, PACK, P])
         for s in range(PACK):
@@ -141,8 +153,11 @@ def tile_picked_mhhzqsndminpags_none_p_kernel(tc, x_words, x_scales, d_words, d_
         z_turned = [keep.tile([P, 2, 2 * P], BF16, name="z_turned%d" % c) for c in range(2)]
         diff = {}
 
-        def step_one(t):
-            nc.scalar.activation(ds[t][:].indirect(n1_l[:]), h[t][:, :S], COPY)
+        def send(t, lo, hi):
+            nc.scalar.activation(ds[t][:].indirect(n1_l[:, lo // 16 : hi // 16]), h[t][:, lo:hi], COPY)
+
+        def step_one(t, lo):
+            send(t, lo, S)
             nc.scalar.activation(hg[t][:], h[t][:].indirect(n2_l[:]), COPY)
             nc.vector.tensor_tensor(st[t][:, :S], ds[t][:, :S], hg[t][:], ALU.min)
 
@@ -169,21 +184,23 @@ def tile_picked_mhhzqsndminpags_none_p_kernel(tc, x_words, x_scales, d_words, d_
             for c in range(2):
                 turn_diff(t, c)
 
-        step_one(0)
-        step_one(1)
-        first_products(2, words_b, plane_b)
-        first_products(3, words_b, plane_b)
-        d3_bytes = keep.tile([P, H], U8, align_bytes=64, tag="words_d")
-        d3_words = keep.tile([P, H], U32, align_bytes=64, tag="words_x")
+        send(0, 0, HALF)
+        send(1, 0, HALF)
+        step_one(0, HALF)
+        step_one(1, HALF)
+        late_products(2)
+        late_products(3)
+        d3_bytes = keep.tile([P, H], U8, align_bytes=64, tag="words_x0")
+        d3_words = keep.tile([P, H], U32, align_bytes=64, tag="words_x1")
         step_two(0)
         for c in range(2):
             nc.vector.tensor_copy(d3_bytes[:, c * PIECE : (c + 1) * PIECE], d_byte_tab[:].indirect(piece(k3_l, c)))
         place_scale_rows(plane_3, d3_bytes)
-        step_one(2)
+        step_one(2, 0)
         step_two(1)
         for c in range(2):
             nc.vector.tensor_copy(d3_words[:, c * PIECE : (c + 1) * PIECE], d_word_tab[:].indirect(piece(k3_l, c)))
-        step_one(3)
+        step_one(3, 0)
         step_two(2)
 
         last = TILES - 1

@@ -211,13 +211,19 @@ def tile_picked_mhhzqsndminpags_none_p_kernel(tc, x_words, x_scales, d_words, d_
             turn_diff(last, c)
         z_words = keep.tile([P, S], U32, align_bytes=64)
         z_plane = keep.tile([P, S], U8, align_bytes=64)
-        z = [keep.tile([P, PACK * HALF], BF16, align_bytes=64, name="z%d" % c) for c in range(2)]
+        spans = [slice(0, HALF), slice(HALF, HALF + HALF // 2), slice(HALF + HALF // 2, S)]
+        z = [keep.tile([P, PACK * (span.stop - span.start)], BF16, align_bytes=64, name="z%d" % i) for i, span in enumerate(spans)]
+        backs = []
         for c in range(2):
             back = bank(6 + c, [P, 2, HALF])
             pairs = z_turned[c][:].bitcast(F32)
             for u in range(2):
                 nc.tensor.transpose(back[:, u, :], pairs[:, u, :], ident[:])
-            nc.scalar.copy(z[c][:].bitcast(F32).rearrange("p (j u) -> p j u", u=2), back[:].rearrange("p u j -> p j u"))
+            backs.append(back)
+        for i, span in enumerate(spans):
+            c = span.start // HALF
+            nc.scalar.copy(z[i][:].bitcast(F32).rearrange("p (j u) -> p j u", u=2), backs[c][:, :, span.start - c * HALF : span.stop - c * HALF].rearrange("p u j -> p j u"))
+
         def last_product(t, cols, number):
             acc = bank(number, [P, cols.stop - cols.start])
             nc.tensor.matmul_mx(
@@ -231,12 +237,12 @@ def tile_picked_mhhzqsndminpags_none_p_kernel(tc, x_words, x_scales, d_words, d_
             )
             nc.vector.tensor_scalar(h2[t][:, cols], acc[:], 0.0625, None, ALU.mult)
 
-        for c in range(2):
-            nc.vector.quantize_mx(out=z_words[:, c * HALF : (c + 1) * HALF].bitcast(FP8X4), scales=z_plane[:, c * HALF : (c + 1) * HALF], in_=z[c][:])
-        for c in range(2):
-            last_product(0, slice(c * HALF, (c + 1) * HALF), c)
+        for i, span in enumerate(spans):
+            nc.vector.quantize_mx(out=z_words[:, span].bitcast(FP8X4), scales=z_plane[:, span], in_=z[i][:])
+        for i, span in enumerate(spans):
+            last_product(0, span, i)
         for t in range(1, TILES):
-            last_product(t, slice(0, S), 1 + t)
+            last_product(t, slice(0, S), 2 + t)
 
         h2g = [keep.tile([P, S], F32, name="h2g%d" % t) for t in range(TILES)]
         nw = [keep.tile([P, S], F32, name="nw%d" % t) for t in range(TILES)]

from contextlib import ExitStack

import concourse.mybir as mybir
from concourse.masks import make_identity

K, T, S, G, H, U = 512, 1024, 256, 2048, 512, 1024
FLOPS = 3 * 2 * K * H * S

F32 = mybir.dt.float32
BF16 = mybir.dt.bfloat16
I32 = mybir.dt.int32
U32 = mybir.dt.uint32
U16 = mybir.dt.uint16
U8 = mybir.dt.uint8
FP8X4 = mybir.dt.float8_e4m3fn_x4
ALU = mybir.AluOpType
COPY = mybir.ActivationFunctionType.Copy

P = 128
PACK = 4
TILES = H // P
GATHER_W = S + 16
SCATTER_W = S + 128
HALF = S // 2
PIECE = H // 2


def tile_picked_mhhzqsndminpags_none_p_kernel(tc, x_words, x_scales, d_words, d_scales, gs, offs, k1, hz, k2, n1, n2, n3, k3, n4, n5, out):
    nc = tc.nc
    with ExitStack() as ctx:
        lists = ctx.enter_context(tc.tile_pool(name="lists", bufs=1))
        keep = ctx.enter_context(tc.tile_pool(name="keep", bufs=1))
        psum = ctx.enter_context(tc.psum_pool(name="psum", bufs=1))

        def load_list(src, name):
            tile = lists.tile([P, src.shape[1]], U16, name=name)
            nc.sync.dma_start(tile[:], src)
            return tile

        def place_scale_rows(plane, gathered):
            for q in range(4):
                nc.sync.dma_start(plane[32 * q : 32 * q + 4, :].bitcast(I32), gathered[32 * q : 32 * q + 32 : 8, :].bitcast(I32))

        def bank(number, shape):
            return psum.tile(shape, F32, name="bank", tag="bank%d" % number)

        d_byte_tab = keep.tile([P, G], U8, align_bytes=64)
        x_byte_tab = keep.tile([P, T], U8, align_bytes=64)
        nc.sync.dma_start(x_byte_tab[:].bitcast(I32), x_scales[0].bitcast(I32).unsqueeze(1).to_broadcast([16, 8, T // 4]))
        offs_l = load_list(offs, "offs_l")
        hz_l = load_list(hz, "hz_l")
        nc.sync.dma_start(d_byte_tab[:].bitcast(I32), d_scales[0].bitcast(I32).unsqueeze(1).to_broadcast([16, 8, G // 4]))
        k1_l = load_list(k1, "k1_l")
        k2_l = load_list(k2, "k2_l")
        d_word_tab = keep.tile([P, G], U32, align_bytes=64)
        x_word_tab = keep.tile([P, T], U32, align_bytes=64)
        nc.sync.dma_start(d_word_tab[:].bitcast(I32), d_words[0].rearrange("p n t -> p (n t)").bitcast(I32))
        n1_l = load_list(n1, "n1_l")
        n2_l = load_list(n2, "n2_l")
        n3_l = load_list(n3, "n3_l")
        k3_l = load_list(k3, "k3_l")
        nc.sync.dma_start(x_word_tab[:].bitcast(I32), x_words[0].rearrange("p n t -> p (n t)").bitcast(I32))
        n5_l = load_list(n5, "n5_l")
        n4_l = load_list(n4, "n4_l")
        gain = keep.tile([P, PACK], F32)
        nc.sync.dma_start(gain[:], gs.rearrange("(p s) o -> p (s o)", s=PACK))

        plane_a = keep.tile([P, 2 * S + 2 * PIECE], U8, align_bytes=64)
        plane_b = keep.tile([P, 2 * PIECE], U8, align_bytes=64)
        plane_3 = keep.tile([P, H], U8, align_bytes=64)
        for plane in (plane_a, plane_b, plane_3):
            nc.vector.memset(plane[:].bitcast(I32), 0)

        pages = [keep.tile([P, U], F32, name="page%d" % t) for t in range(TILES)]
        nc.vector.memset(pages[0][:], 0.0)
        for t in range(1, TILES):
            nc.scalar.copy(pages[t][:], pages[0][:])

        ident = keep.tile([P, P], F32)
        make_identity(nc, ident[:])
        h = [keep.tile([P, GATHER_W], F32, name="h%d" % t) for t in range(TILES)]
        st = [keep.tile([P, GATHER_W], F32, name="st%d" % t) for t in range(TILES)]
        h2 = [keep.tile([P, GATHER_W], F32, name="h2%d" % t) for t in range(TILES)]
        for tile in h + st + h2:
            nc.gpsimd.memset(tile[:, S:], 0.0)

        def piece(tile, c):
            return tile[:, c * PIECE // 16 : (c + 1) * PIECE // 16]

        def half(tile, c):
            return tile[:, c * HALF // 16 : (c + 1) * HALF // 16]

        bytes_a = keep.tile([P, 2 * S + 2 * PIECE], U8, align_bytes=64)
        nc.vector.tensor_copy(bytes_a[:, :S], x_byte_tab[:].indirect(offs_l[:]))
        nc.vector.tensor_copy(bytes_a[:, S : 2 * S], x_byte_tab[:].indirect(hz_l[:]))
        nc.vector.tensor_copy(bytes_a[:, 2 * S : 2 * S + PIECE], d_byte_tab[:].indirect(piece(k1_l, 0)))
        nc.vector.tensor_copy(bytes_a[:, 2 * S + PIECE :], d_byte_tab[:].indirect(piece(k2_l, 0)))
        place_scale_rows(plane_a, bytes_a)

        x_picked = [keep.tile([P, 2 * HALF], U32, align_bytes=64, name="x_picked", tag="words_x%d" % c) for c in range(2)]
        words_a = [keep.tile([P, PIECE], U32, align_bytes=64, name="words_a", tag="words_d%d" % l) for l in range(2)]
        nc.vector.tensor_copy(words_a[0][:], d_word_tab[:].indirect(piece(k1_l, 0)))
        nc.vector.tensor_copy(words_a[1][:], d_word_tab[:].indirect(piece(k2_l, 0)))
        for c in range(2):
            nc.vector.tensor_copy(x_picked[c][:, :HALF], x_word_tab[:].indirect(half(offs_l, c)))
            nc.vector.tensor_copy(x_picked[c][:, HALF:], x_word_tab[:].indirect(half(hz_l, c)))

        def first_products(t, c, acc, words, scales):
            for l in range(2):
                nc.tensor.matmul_mx(
                    out=acc,
                    lhsT=words[l][:, (t % 2) * P : (t % 2 + 1) * P].bitcast(FP8X4),
                    lhsT_scale=scales[:, l * PIECE + (t % 2) * P : l * PIECE + (t % 2 + 1) * P],
                    rhs=x_picked[c][:, l * HALF : (l + 1) * HALF].bitcast(FP8X4),
                    rhs_scale=plane_a[:, l * S + c * HALF : l * S + (c + 1) * HALF],
                    start=(l == 0),
                    stop=(l == 1),
                )

        for c in range(2):
            for t in range(2):
                acc = bank(4 * c + t, [P, HALF])
                first_products(t, c, acc[:], words_a, plane_a[:, 2 * S :])
                if t == 0 and c == 0:
                    nc.scalar.activation(h[t][:, :HALF], acc[:], COPY, scale=0.0625)
                else:
                    nc.vector.tensor_scalar(h[t][:, c * HALF : (c + 1) * HALF], acc[:], 0.0625, None, ALU.mult)

        def late_products(t):
            acc = bank(t, [P, S])
            for c in range(2):
                first_products(t, c, acc[:, c * HALF : (c + 1) * HALF], words_b, plane_b)
            nc.vector.tensor_scalar(h[t][:, :S], acc[:], 0.0625, None, ALU.mult)

        bytes_b = keep.tile([P, 2 * PIECE], U8, align_bytes=64, tag="words_d0")
        nc.vector.tensor_copy(bytes_b[:, :PIECE], d_byte_tab[:].indirect(piece(k1_l, 1)))
        nc.vector.tensor_copy(bytes_b[:, PIECE:], d_byte_tab[:].indirect(piece(k2_l, 1)))
        place_scale_rows(plane_b, bytes_b)
        both_b = keep.tile([P, 2 * PIECE], U32, align_bytes=64, tag="words_d1")
        words_b = [both_b[:, :PIECE], both_b[:, PIECE:]]
        nc.vector.tensor_copy(words_b[0], d_word_tab[:].indirect(piece(k1_l, 1)))
        nc.vector.tensor_copy(words_b[1], d_word_tab[:].indirect(piece(k2_l, 1)))

        gain_bank = bank(1, [P, PACK, P])
        for s in range(PACK):
            nc.tensor.transpose(gain_bank[:, s, :], gain[:, s : s + 1].to_broadcast([P, P]), ident[:])
        gain_row = keep.tile([P, TILES, 2, 32, 2], F32)
        nc.vector.tensor_copy(gain_row[:], gain_bank[:].rearrange("m (u e) (t q) -> m t u q e", u=2, t=TILES))

        ds = [keep.tile([P, SCATTER_W], F32, name="ds%d" % t) for t in range(TILES)]
        hg = [keep.tile([P, S], F32, name="hg%d" % t) for t in range(TILES)]
        neg_stg = [keep.tile([P, S], F32, name="neg_stg%d" % t) for t in range(TILES)]
        z_turned = [keep.tile([P, 2, 2 * P], BF16, name="z_turned%d" % c) for c in range(2)]
        diff = {}

        def send(t, lo, hi):
            nc.scalar.activation(ds[t][:].indirect(n1_l[:, lo // 16 : hi // 16]), h[t][:, lo:hi], COPY)

        def step_one(t, lo):
            send(t, lo, S)
            nc.scalar.activation(hg[t][:], h[t][:].indirect(n2_l[:]), COPY)
            nc.vector.tensor_tensor(st[t][:, :S], ds[t][:, :S], hg[t][:], ALU.min)

        def fetch_st(t, lo, hi):
            nc.scalar.activation(neg_stg[t][:, lo:hi], st[t][:].indirect(n3_l[:, lo // 16 : hi // 16]), COPY, scale=-1.0)

        def turn_st(t, c):
            diff[t, c] = bank((2, 2, 0, 4)[t] + c, [P, P])
            nc.tensor.matmul(diff[t, c][:], st[t][:, c * HALF : (c + 1) * HALF], ident[:], start=True, stop=False, is_transpose=True)

        def turn_diff(t, c):
            nc.tensor.matmul(diff[t, c][:], neg_stg[t][:, c * HALF : (c + 1) * HALF], ident[:], start=False, stop=True, is_transpose=True)
            nc.vector.tensor_tensor(
                z_turned[c][:, :, 64 * t : 64 * (t + 1)].rearrange("j u (q e) -> j u q e", e=2),
                diff[t, c][:].rearrange("j (q u e) -> j u q e", u=2, e=2),
                gain_row[:, t],
                ALU.mult,
            )

        def step_two(t):
            fetch_st(t, 0, S)
            for c in range(2):
                turn_st(t, c)
            for c in range(2):
                turn_diff(t, c)

        send(0, 0, HALF)
        send(1, 0, HALF)
        step_one(0, HALF)
        step_one(1, HALF)
        late_products(2)
        late_products(3)
        d3_bytes = keep.tile([P, H], U8, align_bytes=64, tag="words_x0")
        d3_words = keep.tile([P, H], U32, align_bytes=64, tag="words_x1")
        step_two(0)
        for c in range(2):
            nc.vector.tensor_copy(d3_bytes[:, c * PIECE : (c + 1) * PIECE], d_byte_tab[:].indirect(piece(k3_l, c)))
        place_scale_rows(plane_3, d3_bytes)
        step_one(2, 0)
        step_two(1)
        for c in range(2):
            nc.vector.tensor_copy(d3_words[:, c * PIECE : (c + 1) * PIECE], d_word_tab[:].indirect(piece(k3_l, c)))
        step_one(3, 0)
        step_two(2)

        last = TILES - 1
        for c in range(2):
            turn_st(last, c)
        for c in range(2):
            fetch_st(last, c * HALF, (c + 1) * HALF)
            turn_diff(last, c)
        z_words = keep.tile([P, S], U32, align_bytes=64)
        z_plane = keep.tile([P, S], U8, align_bytes=64)
        spans = [slice(0, HALF), slice(HALF, HALF + HALF // 2), slice(HALF + HALF // 2, S)]
        z = [keep.tile([P, PACK * (span.stop - span.start)], BF16, align_bytes=64, name="z%d" % i) for i, span in enumerate(spans)]
        backs = []
        for c in range(2):
            back = bank(6 + c, [P, 2, HALF])
            pairs = z_turned[c][:].bitcast(F32)
            for u in range(2):
                nc.tensor.transpose(back[:, u, :], pairs[:, u, :], ident[:])
            backs.append(back)
        for i, span in enumerate(spans):
            c = span.start // HALF
            nc.scalar.copy(z[i][:].bitcast(F32).rearrange("p (j u) -> p j u", u=2), backs[c][:, :, span.start - c * HALF : span.stop - c * HALF].rearrange("p u j -> p j u"))

        def last_product(t, cols, number):
            acc = bank(number, [P, cols.stop - cols.start])
            nc.tensor.matmul_mx(
                out=acc[:],
                lhsT=d3_words[:, t * P : (t + 1) * P].bitcast(FP8X4),
                lhsT_scale=plane_3[:, t * P : (t + 1) * P],
                rhs=z_words[:, cols].bitcast(FP8X4),
                rhs_scale=z_plane[:, cols],
                start=True,
                stop=True,
            )
            nc.vector.tensor_scalar(h2[t][:, cols], acc[:], 0.0625, None, ALU.mult)

        for i, span in enumerate(spans):
            nc.vector.quantize_mx(out=z_words[:, span].bitcast(FP8X4), scales=z_plane[:, span], in_=z[i][:])
        for i, span in enumerate(spans):
            last_product(0, span, i)
        for t in range(1, TILES):
            last_product(t, slice(0, S), 2 + t)

        h2g = [keep.tile([P, S], F32, name="h2g%d" % t) for t in range(TILES)]
        nw = [keep.tile([P, S], F32, name="nw%d" % t) for t in range(TILES)]

        def fetch(t):
            nc.scalar.activation(h2g[t][:], h2[t][:].indirect(n5_l[:]), COPY)
            nc.vector.tensor_tensor(nw[t][:], h2[t][:, :S], h2g[t][:], ALU.max)

        def put(t):
            nc.scalar.activation(pages[t][:].indirect(n4_l[:]), nw[t][:], COPY)
            nc.sync.dma_start(out[t * P : (t + 1) * P, :], pages[t][:])

        fetch(0)
        for t in range(1, TILES):
            fetch(t)
            put(t - 1)
        put(TILES - 1)
